import numpy as np
import ml_dtypes


def mxq(x, axis, fmt="e4m3"):
    dtype, down = {"e4m3": (ml_dtypes.float8_e4m3fn, 7), "e5m2": (ml_dtypes.float8_e5m2, 14)}[fmt]
    v = np.moveaxis(np.asarray(x, np.float32).astype(ml_dtypes.bfloat16).astype(np.float64), axis, -1)
    blocks = v.reshape(v.shape[:-1] + (-1, 32))
    amax = np.abs(blocks).max(-1, keepdims=True)
    byte = np.maximum(np.where(amax > 0, np.frexp(amax)[1] - 1 + 127, 0) - down, 1)
    scale = np.exp2(byte - 127.0)
    codes = (blocks / scale).astype(np.float32).astype(dtype).astype(np.float64)
    return np.moveaxis((codes * scale).reshape(v.shape), -1, axis)


WIDE = False


def mx_kscale(k):
    if not WIDE:
        return np.ones(k)
    levels = np.array([30, -30])
    if k % 512:
        return np.exp2(np.random.permutation(np.resize(levels, k // 32))).repeat(32)
    a = np.empty((k // 512, 16))
    for p in range(k // 512):
        a[p, :8] = np.random.permutation(np.resize(levels, 8))
        for g in range(8):
            far = levels[np.abs(levels - a[p, g]) >= 10]
            a[p, g + 8] = far[np.random.randint(len(far))]
    return np.exp2(a.ravel()).repeat(32)


def f64(x):
    return np.asarray(x).astype(np.float64)


def striped(idx):
    return np.tile(np.asarray(idx).reshape(-1, 16).T, (8, 1)).astype(np.uint16)


def unstriped(offs):
    return offs[:16].T.reshape(-1).astype(np.int64)


E2M1 = np.array([0.0, 0.5, 1.0, 1.5, 2.0, 3.0, 4.0, 6.0, -0.0, -0.5, -1.0, -1.5, -2.0, -3.0, -4.0, -6.0])


def pack_weight(w, fmt):
    k, n = w.shape
    w = f64(np.asarray(w, np.float32).astype(ml_dtypes.bfloat16)).reshape(k // 32, 32, n)
    amax = np.abs(w).max(1)
    if fmt in ("e4m3", "e5m2"):
        byte = np.frexp(amax)[1] - 1 + 127 - (7 if fmt == "e4m3" else 14)
    else:
        mant, ex = np.frexp(amax / 6.0)
        byte = np.where(mant > 0.5, ex, ex - 1) + 127
    byte = np.clip(np.where(amax > 0, byte, 1), 1, 254)
    scaled = (w * np.exp2(127.0 - byte)[:, None, :]).reshape(k, n).astype(np.float32)
    by_word = np.ascontiguousarray(scaled.reshape(k // 512, 128, 4, n).transpose(0, 1, 3, 2))
    if fmt in ("e4m3", "e5m2"):
        words = by_word.astype(ml_dtypes.float8_e4m3fn if fmt == "e4m3" else ml_dtypes.float8_e5m2).view(np.uint8)
    else:
        c = by_word.astype(ml_dtypes.float4_e2m1fn).view(np.uint8) & 0xF
        words = (c[..., 0::2] | (c[..., 1::2] << 4)).reshape(k // 512, 128, 2 * n)
    return np.ascontiguousarray(words), np.ascontiguousarray(byte.astype(np.uint8).reshape(k // 512, 16, n))


def unpack_weight(words, scales, fmt):
    g, _, n = scales.shape
    words = np.ascontiguousarray(words).reshape(g, 128, n, -1)
    if fmt in ("e4m3", "e5m2"):
        vals = words.view(ml_dtypes.float8_e4m3fn if fmt == "e4m3" else ml_dtypes.float8_e5m2).astype(np.float64)
    else:
        nib = np.empty((g, 128, n, 4), np.uint8)
        nib[..., 0::2] = words & 0xF
        nib[..., 1::2] = words >> 4
        vals = E2M1[nib]
    vals = vals * np.repeat(np.exp2(scales.astype(np.float64) - 127.0), 8, axis=1)[..., None]
    return vals.transpose(0, 1, 3, 2).reshape(g * 512, n)


def bf(x):
    return np.asarray(x, np.float32).astype(ml_dtypes.bfloat16)


def planes(Y):
    r, m = Y.shape
    b = f64(bf(Y)).reshape(r // 32, 32, m)
    amax = np.abs(b).max(1)
    byte = np.clip(np.where(amax > 0, np.frexp(amax)[1] - 1 + 127 - 7, 1), 1, 254)
    codes = (b * np.exp2(127.0 - byte)[:, None, :]).reshape(r, m).astype(np.float32).astype(ml_dtypes.float8_e4m3fn).view(np.uint8)
    words = codes.reshape(r // 512, 128, 4, m).transpose(0, 1, 3, 2)
    return np.ascontiguousarray(words), np.ascontiguousarray(byte.astype(np.uint8).reshape(r // 512, 16, m))


K, T, J, R, F, Z, N, C = 512, 512, 256, 512, 512, 1024, 512, 1024


def setup_inputs():
    n = np.random.standard_normal
    idx = np.random.permutation(T)[:J]
    idx2 = np.random.permutation(Z)[:J]
    idx3 = np.random.permutation(C)[:J]
    fk = mx_kscale(K)
    fr = mx_kscale(R)
    ff = mx_kscale(F)
    wp = pack_weight(n((K, R)) * 1 / np.sqrt(K) * fk[:, None] * fr, "e5m2")
    xop = pack_weight(n((F, Z)) / ff[:, None], "e5m2")
    w2p = pack_weight(n((F, R)) * 1 / np.sqrt(F) * ff[:, None] * fr, "e4m3")
    wbp = pack_weight(n((R, N)) * 1 / np.sqrt(R) / fr[:, None], "e2m1")
    return {
        "xf": (n((K, T))).astype(np.float32),
        "ow": (n((K, J)) * 0.7).astype(np.float32),
        "fk": (np.random.uniform(0.5, 2.0, (K, 1)) / fk[:, None]).astype(np.float32),
        "w_words": wp[0],
        "w_scales": wp[1],
        "xo_words": xop[0],
        "xo_scales": xop[1],
        "w2_words": w2p[0],
        "w2_scales": w2p[1],
        "wb_words": wbp[0],
        "wb_scales": wbp[1],
        "old": (1.0 * n((N, C))).astype(np.float32),
        "offs": striped(idx),
        "offs2": striped(idx2),
        "offs3": striped(idx3),
    }


def reference(xf, ow, fk, w_words, w_scales, xo_words, xo_scales, w2_words, w2_scales, wb_words, wb_scales, old, offs, offs2, offs3):
    idx = unstriped(offs)
    idx2 = unstriped(offs2)
    idx3 = unstriped(offs3)
    wu = unpack_weight(w_words, w_scales, "e5m2")
    xou = unpack_weight(xo_words, xo_scales, "e5m2")
    w2u = unpack_weight(w2_words, w2_scales, "e4m3")
    wbu = unpack_weight(wb_words, wb_scales, "e2m1")
    u = (f64(xf)[:, idx] - f64(ow)) * f64(fk)
    uq = mxq(u, 0, "e5m2")
    a = wu.T @ uq
    xoidx2g = xou[:, idx2]
    q = w2u.T @ xoidx2g
    hid = np.abs(a - q)
    hidq = mxq(hid, 0, "e5m2")
    p = wbu.T @ hidq
    pp = np.zeros((N, C))
    pp[:, idx3] = p
    y = pp + 0.5 * f64(old)
    words, scales = planes(y)
    return y, words, scales

@@ -1,0 +1,195 @@
+from contextlib import ExitStack
+
+import concourse.mybir as mybir
+
+K, T, J, R, F, Z, N, C = 512, 512, 256, 512, 512, 1024, 512, 1024
+FLOPS = 2 * J * (K * R + F * R + R * N)
+
+F32 = mybir.dt.float32
+BF16 = mybir.dt.bfloat16
+I32 = mybir.dt.int32
+U32 = mybir.dt.uint32
+U16 = mybir.dt.uint16
+U8 = mybir.dt.uint8
+E4M3 = mybir.dt.float8_e4m3fn_x4
+E5M2 = mybir.dt.float8_e5m2_x4
+E2M1 = mybir.dt.float4_e2m1fn_x4
+ALU = mybir.AluOpType
+ACT = mybir.ActivationFunctionType
+
+P = 128
+PACK = 4
+HALF = J // 2
+CHUNK = 256
+
+
+def load_scales(queue, plane, scales):
+    rows = scales[0].bitcast(I32)
+    for q in range(4):
+        quad = rows[4 * q : 4 * q + 4, :].unsqueeze(0).to_broadcast([8, 4, rows.shape[1]])
+        queue.dma_start(out=plane[32 * q : 32 * q + 32, :].bitcast(I32), in_=quad)
+
+
+def deal(copy, dst, src, run):
+    copy(out=dst.rearrange("p (t c i) -> p c t i", t=PACK, i=run), in_=src.rearrange("p (c i t) -> p c t i", t=PACK, i=run))
+
+
+def tile_list_two_offsetpicks_other_absgap_scattered_pl_kernel(
+    tc, xf, ow, fk, w_words, w_scales, xo_words, xo_scales, w2_words, w2_scales, wb_words, wb_scales, old, offs, offs2, offs3,
+    out_0, out_1, out_2,
+):
+    nc = tc.nc
+    with ExitStack() as ctx:
+        sb = ctx.enter_context(tc.tile_pool(name="sb", bufs=1))
+        ps = ctx.enter_context(tc.psum_pool(name="ps", bufs=1))
+
+        def tile(shape, dtype, name):
+            return sb.tile(shape, dtype, name=name, align_bytes=64)
+
+        o1 = tile([P, J // 16], U16, "o1")
+        o2 = tile([P, J // 16], U16, "o2")
+        o3 = tile([P, J // 16], U16, "o3")
+        x_sb = tile([P, PACK, T], F32, "x_sb")
+        ow_sb = tile([P, PACK, J], F32, "ow_sb")
+        fk_sb = tile([P, PACK], F32, "fk_sb")
+        w_raw = tile([P, R], U32, "w_raw")
+        w2_raw = tile([P, R], U32, "w2_raw")
+        wb_raw = tile([P, 2 * N], U8, "wb_raw")
+        xo_raw = tile([P, Z], U32, "xo_raw")
+        ws_raw = tile([P, R], U8, "ws_raw")
+        w2s_raw = tile([P, R], U8, "w2s_raw")
+        wbs_raw = tile([P, N], U8, "wbs_raw")
+        xs_raw = tile([P, Z], U8, "xs_raw")
+        old_sb = tile([P, PACK, C], F32, "old_sb")
+        page = [tile([P, C], F32, f"page{t}") for t in range(PACK)]
+
+        def rows4(ap):
+            return ap.rearrange("(p t) c -> p t c", t=PACK)
+
+        def words(ap):
+            return ap[0].rearrange("p n t -> p (n t)").bitcast(I32)
+
+        nc.sync.dma_start(o1[:], offs)
+        nc.sync.dma_start(o2[:], offs2)
+        nc.sync.dma_start(out=x_sb[:], in_=rows4(xf))
+        nc.sync.dma_start(out=ow_sb[:], in_=rows4(ow))
+        load_scales(nc.scalar, xs_raw, xo_scales)
+        load_scales(nc.scalar, w2s_raw, w2_scales)
+        load_scales(nc.scalar, ws_raw, w_scales)
+        nc.sync.dma_start(out=fk_sb[:], in_=fk.rearrange("(p t) o -> p (t o)", t=PACK))
+        nc.sync.dma_start(out=xo_raw[:].bitcast(I32), in_=words(xo_words))
+        nc.sync.dma_start(out=w2_raw[:].bitcast(I32), in_=words(w2_words))
+        nc.sync.dma_start(out=w_raw[:].bitcast(I32), in_=words(w_words))
+        nc.sync.dma_start(out=wb_raw[:].bitcast(I32), in_=wb_words[0].bitcast(I32))
+        load_scales(nc.sync, wbs_raw, wb_scales)
+        nc.sync.dma_start(o3[:], offs3)
+        nc.sync.dma_start(out=old_sb[:], in_=rows4(old))
+
+        for t in range(PACK):
+            nc.vector.memset(page[t][:], 0.0)
+
+        ws = tile([P, R], U8, "ws")
+        w2s = tile([P, R], U8, "w2s")
+        wbs = tile([P, N], U8, "wbs")
+        w_c = tile([P, R], U32, "w_c")
+        w2_c = tile([P, R], U32, "w2_c")
+        wb_c = tile([P, 2 * N], U8, "wb_c")
+        xo_c = tile([P, J], U32, "xo_c")
+        xs = tile([P, J], U8, "xs")
+        nc.vector.tensor_copy(xs[:], xs_raw[:].indirect(o2[:]))
+
+        picked = tile([P, PACK, J], F32, "picked")
+        for t in range(PACK):
+            if t < 2:
+                nc.vector.tensor_copy(picked[:, t, :], x_sb[:, t, :].indirect(o1[:]))
+            else:
+                nc.scalar.activation(picked[:, t, :], x_sb[:, t, :].indirect(o1[:]), ACT.Copy)
+
+        u_c = [tile([P, HALF], U32, f"u_c{h}") for h in range(2)]
+        u_s = [tile([P, HALF], U8, f"u_s{h}") for h in range(2)]
+        u_bf = [tile([P, HALF * PACK], BF16, f"u_bf{h}") for h in range(2)]
+
+        def centre_and_scale(h):
+            cols = slice(h * HALF, (h + 1) * HALF)
+            diff = tile([P, PACK, HALF], F32, f"diff{h}")
+            nc.vector.tensor_tensor(diff[:], ow_sb[:, :, cols], picked[:, :, cols], ALU.subtract)
+            nc.vector.tensor_tensor(
+                u_bf[h][:].rearrange("p (c i t) -> p c t i", t=PACK, i=4),
+                diff[:].rearrange("p t (c i) -> p c t i", i=4),
+                fk_sb[:].unsqueeze(1).unsqueeze(3).to_broadcast([P, HALF // 4, PACK, 4]),
+                ALU.mult,
+            )
+
+        centre_and_scale(0)
+        nc.vector.tensor_copy(xo_c[:], xo_raw[:].indirect(o2[:]))
+        nc.vector.quantize_mx(out=u_c[0][:].bitcast(E5M2), scales=u_s[0][:], in_=u_bf[0][:])
+        deal(nc.vector.tensor_copy, w2s[:], w2s_raw[:], 16)
+        deal(nc.vector.tensor_copy, ws[:], ws_raw[:], 16)
+        centre_and_scale(1)
+        deal(nc.vector.tensor_copy, wbs[:], wbs_raw[:], 16)
+        nc.vector.quantize_mx(out=u_c[1][:].bitcast(E5M2), scales=u_s[1][:], in_=u_bf[1][:])
+        deal(nc.scalar.copy, w2_c[:], w2_raw[:], 4)
+        deal(nc.scalar.copy, w_c[:], w_raw[:], 4)
+        deal(nc.scalar.copy, wb_c[:].bitcast(U16), wb_raw[:].bitcast(U16), 8)
+
+        gap = [ps.tile([P, PACK, HALF], F32, name=f"gap{h}") for h in range(2)]
+        for h in range(2):
+            cols = slice(h * HALF, (h + 1) * HALF)
+            for t in range(PACK):
+                m = slice(t * P, (t + 1) * P)
+                nc.tensor.matmul_mx(
+                    out=gap[h][:, t, :], lhsT=w2_c[:, m].bitcast(E4M3), lhsT_scale=w2s[:, m],
+                    rhs=xo_c[:, cols].bitcast(E5M2), rhs_scale=xs[:, cols], start=(t == 0), stop=False,
+                )
+        p_sb = []
+        for h in range(2):
+            for t in range(PACK):
+                m = slice(t * P, (t + 1) * P)
+                nc.tensor.matmul_mx(
+                    out=gap[h][:, t, :], lhsT=w_c[:, m].bitcast(E5M2), lhsT_scale=ws[:, m],
+                    rhs=u_c[h][:].bitcast(E5M2), rhs_scale=u_s[h][:], start=False, stop=(t == PACK - 1),
+                )
+        for h in range(2):
+            hid_bf = tile([P, HALF, PACK], BF16, f"hid_bf{h}")
+            nc.scalar.activation(hid_bf[:], gap[h][:].rearrange("p t j -> p j t"), ACT.Abs)
+            hid_c = tile([P, HALF], U32, f"hid_c{h}")
+            hid_s = tile([P, HALF], U8, f"hid_s{h}")
+            nc.vector.quantize_mx(out=hid_c[:].bitcast(E5M2), scales=hid_s[:], in_=hid_bf[:].rearrange("p j t -> p (j t)"))
+            prod = ps.tile([P, PACK, HALF], F32, name=f"prod{h}")
+            for t in range(PACK):
+                nc.tensor.matmul_mx(
+                    out=prod[:, t, :], lhsT=wb_c[:, 2 * t * P : 2 * (t + 1) * P].bitcast(E2M1), lhsT_scale=wbs[:, t * P : (t + 1) * P],
+                    rhs=hid_c[:].bitcast(E5M2), rhs_scale=hid_s[:], start=True, stop=True,
+                )
+            p_sb.append(tile([P, PACK, HALF], F32, f"p_sb{h}"))
+            if h == 0:
+                nc.vector.tensor_copy(p_sb[h][:], prod[:])
+            else:
+                nc.scalar.copy(p_sb[h][:], prod[:])
+
+        for h in range(2):
+            lst = o3[:, h * HALF // 16 : (h + 1) * HALF // 16]
+            for t in range(PACK):
+                if t < 2:
+                    nc.vector.tensor_copy(page[t][:].indirect(lst), p_sb[h][:, t, :])
+                else:
+                    nc.scalar.activation(page[t][:].indirect(lst), p_sb[h][:, t, :], ACT.Copy)
+
+        y_s = tile([P, C], U8, "y_s")
+        out0_v = out_0.rearrange("(p t) c -> p t c", t=PACK)
+        out1_v = out_1[0].rearrange("p n t -> p (n t)").bitcast(I32)
+        for b in range(C // CHUNK):
+            cols = slice(b * CHUNK, (b + 1) * CHUNK)
+            y = tile([P, PACK, CHUNK], F32, f"y{b}")
+            for t in range(PACK):
+                nc.vector.scalar_tensor_tensor(y[:, t, :], old_sb[:, t, cols], 0.5, page[t][:, cols], ALU.mult, ALU.add)
+            nc.sync.dma_start(out=out0_v[:, :, cols], in_=y[:])
+            y_bf = tile([P, CHUNK * PACK], BF16, f"y_bf{b}")
+            cast = nc.vector.tensor_copy if b == C // CHUNK - 1 else nc.scalar.copy
+            cast(out=y_bf[:].rearrange("p (c i t) -> p c t i", t=PACK, i=4), in_=y[:].rearrange("p t (c i) -> p c t i", i=4))
+            y_c = tile([P, CHUNK], U32, f"y_c{b}")
+            nc.vector.quantize_mx(out=y_c[:].bitcast(E4M3), scales=y_s[:, cols], in_=y_bf[:])
+            nc.sync.dma_start(out=out1_v[:, cols], in_=y_c[:].bitcast(I32))
+        for q in range(4):
+            queue = nc.sync if q % 2 == 0 else nc.scalar
+            queue.dma_start(out=out_2[0, 4 * q : 4 * q + 4, :].bitcast(I32), in_=y_s[32 * q : 32 * q + 4, :].bitcast(I32))

@@ -20,12 +20,13 @@ ACT = mybir.ActivationFunctionType
 P = 128
 PACK = 4
 HALF = J // 2
-CHUNK = 256
+S_PLANES = (1, 2, 3)
+V_PLANES = (0,)
 
 
-def load_scales(queue, plane, scales):
+def load_scales(queue, plane, scales, quads=range(4)):
     rows = scales[0].bitcast(I32)
-    for q in range(4):
+    for q in quads:
         quad = rows[4 * q : 4 * q + 4, :].unsqueeze(0).to_broadcast([8, 4, rows.shape[1]])
         queue.dma_start(out=plane[32 * q : 32 * q + 32, :].bitcast(I32), in_=quad)
 
@@ -60,7 +61,7 @@ def tile_list_two_offsetpicks_other_absgap_scattered_pl_kernel(
         w2s_raw = tile([P, R], U8, "w2s_raw")
         wbs_raw = tile([P, N], U8, "wbs_raw")
         xs_raw = tile([P, Z], U8, "xs_raw")
-        old_sb = tile([P, PACK, C], F32, "old_sb")
+        old_sb = [tile([P, C], F32, f"old{t}") for t in range(PACK)]
         page = [tile([P, C], F32, f"page{t}") for t in range(PACK)]
 
         def rows4(ap):
@@ -75,15 +76,18 @@ def tile_list_two_offsetpicks_other_absgap_scattered_pl_kernel(
         nc.sync.dma_start(out=ow_sb[:], in_=rows4(ow))
         load_scales(nc.scalar, xs_raw, xo_scales)
         load_scales(nc.scalar, w2s_raw, w2_scales)
-        load_scales(nc.scalar, ws_raw, w_scales)
-        nc.sync.dma_start(out=fk_sb[:], in_=fk.rearrange("(p t) o -> p (t o)", t=PACK))
+        nc.gpsimd.dma_start(out=fk_sb[:], in_=fk.rearrange("(p t) o -> p (t o)", t=PACK))
+        load_scales(nc.gpsimd, ws_raw, w_scales, (2, 3))
+        load_scales(nc.sync, ws_raw, w_scales, (0,))
         nc.sync.dma_start(out=xo_raw[:].bitcast(I32), in_=words(xo_words))
         nc.sync.dma_start(out=w2_raw[:].bitcast(I32), in_=words(w2_words))
         nc.sync.dma_start(out=w_raw[:].bitcast(I32), in_=words(w_words))
+        load_scales(nc.sync, ws_raw, w_scales, (1,))
         nc.sync.dma_start(out=wb_raw[:].bitcast(I32), in_=wb_words[0].bitcast(I32))
         load_scales(nc.sync, wbs_raw, wb_scales)
         nc.sync.dma_start(o3[:], offs3)
-        nc.sync.dma_start(out=old_sb[:], in_=rows4(old))
+        for t in range(PACK):
+            nc.sync.dma_start(out=old_sb[t][:], in_=rows4(old)[:, t, :])
 
         for t in range(PACK):
             nc.vector.memset(page[t][:], 0.0)
@@ -155,41 +159,50 @@ def tile_list_two_offsetpicks_other_absgap_scattered_pl_kernel(
             hid_c = tile([P, HALF], U32, f"hid_c{h}")
             hid_s = tile([P, HALF], U8, f"hid_s{h}")
             nc.vector.quantize_mx(out=hid_c[:].bitcast(E5M2), scales=hid_s[:], in_=hid_bf[:].rearrange("p j t -> p (j t)"))
-            prod = ps.tile([P, PACK, HALF], F32, name=f"prod{h}")
-            for t in range(PACK):
-                nc.tensor.matmul_mx(
-                    out=prod[:, t, :], lhsT=wb_c[:, 2 * t * P : 2 * (t + 1) * P].bitcast(E2M1), lhsT_scale=wbs[:, t * P : (t + 1) * P],
-                    rhs=hid_c[:].bitcast(E5M2), rhs_scale=hid_s[:], start=True, stop=True,
-                )
-            p_sb.append(tile([P, PACK, HALF], F32, f"p_sb{h}"))
-            if h == 0:
-                nc.vector.tensor_copy(p_sb[h][:], prod[:])
-            else:
-                nc.scalar.copy(p_sb[h][:], prod[:])
+            prod_s = ps.tile([P, 3, HALF], F32, name=f"prod_s{h}")
+            prod_v = ps.tile([P, 1, HALF], F32, name=f"prod_v{h}")
+            for prod, planes in ((prod_s, S_PLANES), (prod_v, V_PLANES)):
+                for e, t in enumerate(planes):
+                    nc.tensor.matmul_mx(
+                        out=prod[:, e, :], lhsT=wb_c[:, 2 * t * P : 2 * (t + 1) * P].bitcast(E2M1), lhsT_scale=wbs[:, t * P : (t + 1) * P],
+                        rhs=hid_c[:].bitcast(E5M2), rhs_scale=hid_s[:], start=True, stop=True,
+                    )
+            p_sb.append((prod_s, prod_v))
 
+        lst = [o3[:, h * HALF // 16 : (h + 1) * HALF // 16] for h in range(2)]
+        p_s = tile([P, 3, J], F32, "p_s")
+        p_v = tile([P, J], F32, "p_v")
         for h in range(2):
-            lst = o3[:, h * HALF // 16 : (h + 1) * HALF // 16]
-            for t in range(PACK):
-                if t < 2:
-                    nc.vector.tensor_copy(page[t][:].indirect(lst), p_sb[h][:, t, :])
-                else:
-                    nc.scalar.activation(page[t][:].indirect(lst), p_sb[h][:, t, :], ACT.Copy)
+            cols = slice(h * HALF, (h + 1) * HALF)
+            nc.vector.tensor_copy(p_v[:, cols], p_sb[h][1][:, 0, :])
+            nc.vector.tensor_copy(page[0][:].indirect(lst[h]), p_v[:, cols])
+            nc.scalar.copy(p_s[:, :, cols], p_sb[h][0][:])
+            nc.scalar.activation(page[1][:].indirect(lst[h]), p_s[:, 0, cols], ACT.Copy)
+        for e in (1, 2):
+            nc.scalar.activation(page[S_PLANES[e]][:].indirect(o3[:]), p_s[:, e, :], ACT.Copy)
 
+        W = C // 2
+        y = [tile([P, PACK, W], F32, f"y{g}") for g in range(2)]
         y_s = tile([P, C], U8, "y_s")
-        out0_v = out_0.rearrange("(p t) c -> p t c", t=PACK)
-        out1_v = out_1[0].rearrange("p n t -> p (n t)").bitcast(I32)
-        for b in range(C // CHUNK):
-            cols = slice(b * CHUNK, (b + 1) * CHUNK)
-            y = tile([P, PACK, CHUNK], F32, f"y{b}")
-            for t in range(PACK):
-                nc.vector.scalar_tensor_tensor(y[:, t, :], old_sb[:, t, cols], 0.5, page[t][:, cols], ALU.mult, ALU.add)
-            nc.sync.dma_start(out=out0_v[:, :, cols], in_=y[:])
-            y_bf = tile([P, CHUNK * PACK], BF16, f"y_bf{b}")
-            cast = nc.vector.tensor_copy if b == C // CHUNK - 1 else nc.scalar.copy
-            cast(out=y_bf[:].rearrange("p (c i t) -> p c t i", t=PACK, i=4), in_=y[:].rearrange("p t (c i) -> p c t i", i=4))
-            y_c = tile([P, CHUNK], U32, f"y_c{b}")
-            nc.vector.quantize_mx(out=y_c[:].bitcast(E4M3), scales=y_s[:, cols], in_=y_bf[:])
-            nc.sync.dma_start(out=out1_v[:, cols], in_=y_c[:].bitcast(I32))
+        out0_v = rows4(out_0)
+        out1_v = words(out_1)
+        for t in range(PACK):
+            for g in range(2):
+                cols = slice(g * W, (g + 1) * W)
+                nc.vector.scalar_tensor_tensor(y[g][:, t, :], old_sb[t][:, cols], 0.5, page[t][:, cols], ALU.mult, ALU.add)
+                nc.sync.dma_start(out=out0_v[:, t, cols], in_=y[g][:, t, :])
+        spans = [(0, 256), (256, 512), (512, 768), (768, 1024)]
+        y_bf = []
+        for b, (lo, hi) in enumerate(spans):
+            y_bf.append(tile([P, (hi - lo) * PACK], BF16, f"y_bf{b}"))
+            cast = nc.vector.tensor_copy if b >= 2 else nc.scalar.copy
+            g = lo // W
+            cast(out=y_bf[b][:].rearrange("p (c i t) -> p c t i", t=PACK, i=4), in_=y[g][:, :, lo - g * W : hi - g * W].rearrange("p t (c i) -> p c t i", i=4))
+        for b in (2, 0, 3, 1):
+            lo, hi = spans[b]
+            y_c = tile([P, hi - lo], U32, f"y_c{b}")
+            nc.vector.quantize_mx(out=y_c[:].bitcast(E4M3), scales=y_s[:, lo:hi], in_=y_bf[b][:])
+            nc.sync.dma_start(out=out1_v[:, lo:hi], in_=y_c[:].bitcast(I32))
         for q in range(4):
             queue = nc.sync if q % 2 == 0 else nc.scalar
             queue.dma_start(out=out_2[0, 4 * q : 4 * q + 4, :].bitcast(I32), in_=y_s[32 * q : 32 * q + 4, :].bitcast(I32))

from contextlib import ExitStack

import concourse.mybir as mybir

K, T, J, R, F, Z, N, C = 512, 512, 256, 512, 512, 1024, 512, 1024
FLOPS = 2 * J * (K * R + F * R + R * N)

F32 = mybir.dt.float32
BF16 = mybir.dt.bfloat16
I32 = mybir.dt.int32
U32 = mybir.dt.uint32
U16 = mybir.dt.uint16
U8 = mybir.dt.uint8
E4M3 = mybir.dt.float8_e4m3fn_x4
E5M2 = mybir.dt.float8_e5m2_x4
E2M1 = mybir.dt.float4_e2m1fn_x4
ALU = mybir.AluOpType
ACT = mybir.ActivationFunctionType

P = 128
PACK = 4
HALF = J // 2
S_PLANES = (1, 2, 3)
V_PLANES = (0,)


def load_scales(queue, plane, scales, quads=range(4)):
    rows = scales[0].bitcast(I32)
    for q in quads:
        quad = rows[4 * q : 4 * q + 4, :].unsqueeze(0).to_broadcast([8, 4, rows.shape[1]])
        queue.dma_start(out=plane[32 * q : 32 * q + 32, :].bitcast(I32), in_=quad)


def deal(copy, dst, src, run):
    copy(out=dst.rearrange("p (t c i) -> p c t i", t=PACK, i=run), in_=src.rearrange("p (c i t) -> p c t i", t=PACK, i=run))


def tile_list_two_offsetpicks_other_absgap_scattered_pl_kernel(
    tc, xf, ow, fk, w_words, w_scales, xo_words, xo_scales, w2_words, w2_scales, wb_words, wb_scales, old, offs, offs2, offs3,
    out_0, out_1, out_2,
):
    nc = tc.nc
    with ExitStack() as ctx:
        sb = ctx.enter_context(tc.tile_pool(name="sb", bufs=1))
        ps = ctx.enter_context(tc.psum_pool(name="ps", bufs=1))

        def tile(shape, dtype, name):
            return sb.tile(shape, dtype, name=name, align_bytes=64)

        o1 = tile([P, J // 16], U16, "o1")
        o2 = tile([P, J // 16], U16, "o2")
        o3 = tile([P, J // 16], U16, "o3")
        x_sb = tile([P, PACK, T], F32, "x_sb")
        ow_sb = tile([P, PACK, J], F32, "ow_sb")
        fk_sb = tile([P, PACK], F32, "fk_sb")
        w_raw = tile([P, R], U32, "w_raw")
        w2_raw = tile([P, R], U32, "w2_raw")
        wb_raw = tile([P, 2 * N], U8, "wb_raw")
        xo_raw = tile([P, Z], U32, "xo_raw")
        ws_raw = tile([P, R], U8, "ws_raw")
        w2s_raw = tile([P, R], U8, "w2s_raw")
        wbs_raw = tile([P, N], U8, "wbs_raw")
        xs_raw = tile([P, Z], U8, "xs_raw")
        old_sb = [tile([P, C], F32, f"old{t}") for t in range(PACK)]
        page = [tile([P, C], F32, f"page{t}") for t in range(PACK)]

        def rows4(ap):
            return ap.rearrange("(p t) c -> p t c", t=PACK)

        def words(ap):
            return ap[0].rearrange("p n t -> p (n t)").bitcast(I32)

        nc.sync.dma_start(o1[:], offs)
        nc.sync.dma_start(o2[:], offs2)
        nc.sync.dma_start(out=x_sb[:], in_=rows4(xf))
        nc.sync.dma_start(out=ow_sb[:], in_=rows4(ow))
        load_scales(nc.scalar, xs_raw, xo_scales)
        load_scales(nc.scalar, w2s_raw, w2_scales)
        nc.gpsimd.dma_start(out=fk_sb[:], in_=fk.rearrange("(p t) o -> p (t o)", t=PACK))
        load_scales(nc.gpsimd, ws_raw, w_scales, (2, 3))
        load_scales(nc.sync, ws_raw, w_scales, (0,))
        nc.sync.dma_start(out=xo_raw[:].bitcast(I32), in_=words(xo_words))
        nc.sync.dma_start(out=w2_raw[:].bitcast(I32), in_=words(w2_words))
        nc.sync.dma_start(out=w_raw[:].bitcast(I32), in_=words(w_words))
        load_scales(nc.sync, ws_raw, w_scales, (1,))
        nc.sync.dma_start(out=wb_raw[:].bitcast(I32), in_=wb_words[0].bitcast(I32))
        load_scales(nc.sync, wbs_raw, wb_scales)
        nc.sync.dma_start(o3[:], offs3)
        for t in range(PACK):
            nc.sync.dma_start(out=old_sb[t][:], in_=rows4(old)[:, t, :])

        for t in range(PACK):
            nc.vector.memset(page[t][:], 0.0)

        ws = tile([P, R], U8, "ws")
        w2s = tile([P, R], U8, "w2s")
        wbs = tile([P, N], U8, "wbs")
        w_c = tile([P, R], U32, "w_c")
        w2_c = tile([P, R], U32, "w2_c")
        wb_c = tile([P, 2 * N], U8, "wb_c")
        xo_c = tile([P, J], U32, "xo_c")
        xs = tile([P, J], U8, "xs")
        nc.vector.tensor_copy(xs[:], xs_raw[:].indirect(o2[:]))

        picked = tile([P, PACK, J], F32, "picked")
        for t in range(PACK):
            if t < 2:
                nc.vector.tensor_copy(picked[:, t, :], x_sb[:, t, :].indirect(o1[:]))
            else:
                nc.scalar.activation(picked[:, t, :], x_sb[:, t, :].indirect(o1[:]), ACT.Copy)

        u_c = [tile([P, HALF], U32, f"u_c{h}") for h in range(2)]
        u_s = [tile([P, HALF], U8, f"u_s{h}") for h in range(2)]
        u_bf = [tile([P, HALF * PACK], BF16, f"u_bf{h}") for h in range(2)]

        def centre_and_scale(h):
            cols = slice(h * HALF, (h + 1) * HALF)
            diff = tile([P, PACK, HALF], F32, f"diff{h}")
            nc.vector.tensor_tensor(diff[:], ow_sb[:, :, cols], picked[:, :, cols], ALU.subtract)
            nc.vector.tensor_tensor(
                u_bf[h][:].rearrange("p (c i t) -> p c t i", t=PACK, i=4),
                diff[:].rearrange("p t (c i) -> p c t i", i=4),
                fk_sb[:].unsqueeze(1).unsqueeze(3).to_broadcast([P, HALF // 4, PACK, 4]),
                ALU.mult,
            )

        centre_and_scale(0)
        nc.vector.tensor_copy(xo_c[:], xo_raw[:].indirect(o2[:]))
        nc.vector.quantize_mx(out=u_c[0][:].bitcast(E5M2), scales=u_s[0][:], in_=u_bf[0][:])
        deal(nc.vector.tensor_copy, w2s[:], w2s_raw[:], 16)
        deal(nc.vector.tensor_copy, ws[:], ws_raw[:], 16)
        centre_and_scale(1)
        deal(nc.vector.tensor_copy, wbs[:], wbs_raw[:], 16)
        nc.vector.quantize_mx(out=u_c[1][:].bitcast(E5M2), scales=u_s[1][:], in_=u_bf[1][:])
        deal(nc.scalar.copy, w2_c[:], w2_raw[:], 4)
        deal(nc.scalar.copy, w_c[:], w_raw[:], 4)
        deal(nc.scalar.copy, wb_c[:].bitcast(U16), wb_raw[:].bitcast(U16), 8)

        gap = [ps.tile([P, PACK, HALF], F32, name=f"gap{h}") for h in range(2)]
        for h in range(2):
            cols = slice(h * HALF, (h + 1) * HALF)
            for t in range(PACK):
                m = slice(t * P, (t + 1) * P)
                nc.tensor.matmul_mx(
                    out=gap[h][:, t, :], lhsT=w2_c[:, m].bitcast(E4M3), lhsT_scale=w2s[:, m],
                    rhs=xo_c[:, cols].bitcast(E5M2), rhs_scale=xs[:, cols], start=(t == 0), stop=False,
                )
        p_sb = []
        for h in range(2):
            for t in range(PACK):
                m = slice(t * P, (t + 1) * P)
                nc.tensor.matmul_mx(
                    out=gap[h][:, t, :], lhsT=w_c[:, m].bitcast(E5M2), lhsT_scale=ws[:, m],
                    rhs=u_c[h][:].bitcast(E5M2), rhs_scale=u_s[h][:], start=False, stop=(t == PACK - 1),
                )
        for h in range(2):
            hid_bf = tile([P, HALF, PACK], BF16, f"hid_bf{h}")
            nc.scalar.activation(hid_bf[:], gap[h][:].rearrange("p t j -> p j t"), ACT.Abs)
            hid_c = tile([P, HALF], U32, f"hid_c{h}")
            hid_s = tile([P, HALF], U8, f"hid_s{h}")
            nc.vector.quantize_mx(out=hid_c[:].bitcast(E5M2), scales=hid_s[:], in_=hid_bf[:].rearrange("p j t -> p (j t)"))
            prod_s = ps.tile([P, 3, HALF], F32, name=f"prod_s{h}")
            prod_v = ps.tile([P, 1, HALF], F32, name=f"prod_v{h}")
            for prod, planes in ((prod_s, S_PLANES), (prod_v, V_PLANES)):
                for e, t in enumerate(planes):
                    nc.tensor.matmul_mx(
                        out=prod[:, e, :], lhsT=wb_c[:, 2 * t * P : 2 * (t + 1) * P].bitcast(E2M1), lhsT_scale=wbs[:, t * P : (t + 1) * P],
                        rhs=hid_c[:].bitcast(E5M2), rhs_scale=hid_s[:], start=True, stop=True,
                    )
            p_sb.append((prod_s, prod_v))

        lst = [o3[:, h * HALF // 16 : (h + 1) * HALF // 16] for h in range(2)]
        p_s = tile([P, 3, J], F32, "p_s")
        p_v = tile([P, J], F32, "p_v")
        for h in range(2):
            cols = slice(h * HALF, (h + 1) * HALF)
            nc.vector.tensor_copy(p_v[:, cols], p_sb[h][1][:, 0, :])
            nc.vector.tensor_copy(page[0][:].indirect(lst[h]), p_v[:, cols])
            nc.scalar.copy(p_s[:, :, cols], p_sb[h][0][:])
            nc.scalar.activation(page[1][:].indirect(lst[h]), p_s[:, 0, cols], ACT.Copy)
        for e in (1, 2):
            nc.scalar.activation(page[S_PLANES[e]][:].indirect(o3[:]), p_s[:, e, :], ACT.Copy)

        W = C // 2
        y = [tile([P, PACK, W], F32, f"y{g}") for g in range(2)]
        y_s = tile([P, C], U8, "y_s")
        out0_v = rows4(out_0)
        out1_v = words(out_1)
        for t in range(PACK):
            for g in range(2):
                cols = slice(g * W, (g + 1) * W)
                nc.vector.scalar_tensor_tensor(y[g][:, t, :], old_sb[t][:, cols], 0.5, page[t][:, cols], ALU.mult, ALU.add)
                nc.sync.dma_start(out=out0_v[:, t, cols], in_=y[g][:, t, :])
        spans = [(0, 256), (256, 512), (512, 768), (768, 1024)]
        y_bf = []
        for b, (lo, hi) in enumerate(spans):
            y_bf.append(tile([P, (hi - lo) * PACK], BF16, f"y_bf{b}"))
            cast = nc.vector.tensor_copy if b >= 2 else nc.scalar.copy
            g = lo // W
            cast(out=y_bf[b][:].rearrange("p (c i t) -> p c t i", t=PACK, i=4), in_=y[g][:, :, lo - g * W : hi - g * W].rearrange("p t (c i) -> p c t i", i=4))
        for b in (2, 0, 3, 1):
            lo, hi = spans[b]
            y_c = tile([P, hi - lo], U32, f"y_c{b}")
            nc.vector.quantize_mx(out=y_c[:].bitcast(E4M3), scales=y_s[:, lo:hi], in_=y_bf[b][:])
            nc.sync.dma_start(out=out1_v[:, lo:hi], in_=y_c[:].bitcast(I32))
        for q in range(4):
            queue = nc.sync if q % 2 == 0 else nc.scalar
            queue.dma_start(out=out_2[0, 4 * q : 4 * q + 4, :].bitcast(I32), in_=y_s[32 * q : 32 * q + 4, :].bitcast(I32))
